import numpy as np, ml_dtypes
CORES = [3,5,19,21,35,37,51,53,67,69]
N = 10
import mx_ref
NC, G, MB, ROOT = 512, 4, 2, 2
C = np.float32(0.047)
BF = ml_dtypes.bfloat16
def cut(t, i, w=512):
    return t[:, w * i:w * i + w]
def tile(rs):
    return np.stack(rs, axis=2).reshape(128, -1).astype(BF)
def layer(w, X):
    out = []
    for i in range(G):
        for t in range(len(X)):
            p = mx_ref.matmul(mx_ref.quantize(cut(w, len(X) * i + t)), X[t])
            z = p if t == 0 else z + p
        out.append(z)
    return out
def act(Z):
    return [np.maximum(z, 0) * C for z in Z]
def setup_inputs(rng):
    def f(*shape):
        return mx_ref.flush((rng.standard_normal(shape, dtype=np.float32) * np.exp2(rng.integers(-2, 3, shape[:-1] + (1,)))).astype(BF))
    return {"x": f(N, 128, MB * 4 * NC), "w1": f(N, 128, G * 512), "w2": f(N, 128, 512)}
def setup_inputs_blocks(rng):
    d = setup_inputs(rng)
    for k in ("x", "w1", "w2"): d[k] = mx_ref.spread(d[k], rng, 4)
    return d
def setup_inputs_wide(rng):
    d = setup_inputs(rng)
    for k in ("x", "w1", "w2"): d[k] = mx_ref.flush((d[k].astype(np.float32) * np.exp2(rng.integers(-8, 9, (N, 1, 1))).astype(np.float32)).astype(BF))
    return d
def setup_inputs_zeros(rng):
    d = setup_inputs(rng); v = d["x"].reshape(N, 128, -1, 4).copy()
    v[np.broadcast_to((rng.random((N, 1, v.shape[2], 1)) < 0.33), v.shape)] = 0
    d["x"] = v.reshape(d["x"].shape)
    return d
def reference(x, w1, w2):
    H = [mx_ref.quantize(tile(act(layer(w1[ROOT], [mx_ref.quantize(cut(x[ROOT], m, 4 * NC))])))) for m in range(MB)]
    y = np.zeros((N, 128, MB * NC), np.float32)
    for r in range(N):
        qw = mx_ref.quantize(w2[r])
        for m in range(MB):
            y[r][:, NC * m:NC * m + NC] = mx_ref.matmul(qw, H[m])
    return {"y": y}

@@ -1,0 +1,288 @@
+import numpy as np
+from concourse.bass import DstId, RemoteDMATransfer
+from concourse.mybir import dt, AluOpType, ActivationFunctionType
+
+SIM_CORES = 80
+NC, MB, G = 512, 2, 4
+COLS = MB * NC
+C = float(np.float32(0.047))
+
+CFG = {
+    "chunks": [128, 128, 256, 256, 256],
+    "pieces": [128] * 8,
+    "relays": [0, 1, 2, 3, 4, 5, 0, 1],
+    "calls": [[0], [1], [2, 3], [4, 5], "s", [6, 7], "c"],
+    "relay_on": 2,
+    "mms": [256, 256, 128, 128, 128, 128],
+    "ygroups": [512, 256, 256],
+    "xlate": [0],
+}
+
+
+def cuts(widths):
+    out, a = [], 0
+    for w in widths:
+        out.append((a, a + w))
+        a += w
+    return out
+
+
+CHUNKS = cuts(CFG["chunks"])
+PIECES = cuts(CFG["pieces"])
+MMS = cuts(CFG["mms"])
+TILES = cuts([NC] * MB)
+W1CUT = 3
+
+
+def name(item):
+    return "%s%d_%d" % item
+
+
+CODES = [("c",) + p for p in PIECES]
+ALL_C, ALL_S = ("c", 0, COLS), ("s", 0, COLS)
+
+SCRATCH = {
+    "xt": ("sbuf", [128, 4 * COLS], "bfloat16"),
+    "w1t": ("sbuf", [128, 4 * 128 * G], "bfloat16"),
+    "w2t": ("sbuf", [128, 4 * 128], "bfloat16"),
+    "ht": ("sbuf", [128, 4 * COLS], "bfloat16"),
+    "qx": ("sbuf", [128, COLS], "float8_e4m3fn_x4"),
+    "sx": ("sbuf", [128, COLS], "uint8"),
+    "qw1": ("sbuf", [128, 128 * G], "float8_e4m3fn_x4"),
+    "sw1": ("sbuf", [128, 128 * G], "uint8"),
+    "qw2": ("sbuf", [128, 128], "float8_e4m3fn_x4"),
+    "sw2": ("sbuf", [128, 128], "uint8"),
+    "qh": ("sbuf", [128, COLS], "float8_e4m3fn_x4"),
+    "sh": ("sbuf", [128, COLS], "uint8"),
+    "yt": ("sbuf", [128, COLS], "float32"),
+    "ps": ("psum", [128, 512 * 8], "float32"),
+}
+SEMAPHORES = (["lw1a", "lw1b", "lw2", "qw1a", "qw1b", "qw2s", "sent", "st_sync", "st_scal"]
+              + ["lx%d" % k for k in range(len(CHUNKS))]
+              + ["qx%d" % k for k in range(len(CHUNKS))]
+              + ["z%d_%d" % (k, b) for k in range(len(CHUNKS)) for b in range(G)]
+              + ["act%d" % k for k in range(len(CHUNKS))]
+              + ["qh%d" % k for k in range(len(CHUNKS))]
+              + ["p%d" % k for k in range(8)]
+              + ["cp%d" % k for k in range(8)]
+              + [name(i) for i in CODES + [ALL_C, ALL_S]])
+
+
+def bits(mask):
+    return [1 << i for i in range(16) if mask >> i & 1]
+
+
+def plan(T, topo):
+    root = T.cores[T.root]
+    here = topo.chip(root)
+    off = [c for c in T.cores if topo.chip(c) != here]
+    sib = [c for c in T.cores if topo.chip(c) == here and c != root]
+    near = [c for c in off if topo.die(c) == topo.die(root)]
+    far = [c for c in off if topo.die(c) != topo.die(root)]
+    helpers = [c for c in range(SIM_CORES) if topo.chip(c) == here and c not in T.cores
+               and topo.die(c) == topo.die(root) and all(topo.may_write(c, d) for d in off)]
+    e_off = bits(topo.mask(root, off[0]))
+    e_on = [b for b in bits(topo.mask(root, sib[0])) if b not in e_off]
+    order = near + far
+    relay = [order[i] for i in CFG["relays"]]
+    scale_relays = sib + helpers[:1]
+    calls = {root: []}
+    for call in CFG["calls"]:
+        if call == "s":
+            n = len(e_on) // len(scale_relays)
+            calls[root].append([(ALL_S, [h], e_on[n * i:n * i + n]) for i, h in enumerate(scale_relays)])
+        elif call == "c":
+            calls[root].append([(ALL_C, sib, e_on)])
+        else:
+            n = len(e_off) // len(call)
+            calls[root].append([(CODES[k], [relay[k]], e_off[n * i:n * i + n]) for i, k in enumerate(call)])
+    for k, r in enumerate(relay):
+        on = [c for c in off if c != r and topo.chip(c) == topo.chip(r)]
+        away = [c for c in off if topo.chip(c) != topo.chip(r)]
+        calls.setdefault(r, []).append([(CODES[k], away, e_off), (CODES[k], on, e_on[:CFG["relay_on"]])])
+    for i, h in enumerate(scale_relays):
+        calls.setdefault(h, []).append([(ALL_S, off[i::len(scale_relays)], e_off)])
+    return calls
+
+
+def landings(calls, core):
+    out = {}
+    for L in calls.values():
+        for call in L:
+            for item, dsts, engines in call:
+                for d in dsts:
+                    if d == core:
+                        out[item] = out.get(item, 0) + len(engines)
+    return out
+
+
+def view(T, item):
+    kind, a, b = item
+    return T.qh[:, a:b].bitcast(dt.uint8) if kind == "c" else T.sh[:, a:b]
+
+
+def send(g, T, topo, calls, ready):
+    total = 0
+    for call in calls:
+        transfers = []
+        for item, dsts, engines in call:
+            ready(item)
+            ids = []
+            for d in dsts:
+                rid, pid, _ = topo.addr(d)
+                ids.append(DstId(rid=rid, pnc=pid))
+            transfers.append(RemoteDMATransfer(
+                dst_ids=ids, dma_engine_mask=sum(engines), remote_sem=T.sem[name(item)],
+                srcs=[view(T, item)], dsts=[view(T, item) for _ in dsts]))
+            total += len(engines)
+        g.remote_dma_fused(transfers, local_sem=T.sem.sent)
+    if total:
+        g.wait_ge(T.sem.sent, total)
+
+
+def waiter(queue, T):
+    seen = {}
+
+    def wait(sem, val):
+        if seen.get(sem, 0) < val:
+            seen[sem] = val
+            queue.wait_ge(T.sem[sem], val)
+    return wait
+
+
+def mm(q, T, bank, n, w, sw, x, sx):
+    return q.matmul_mx(T.ps[:, 512 * bank:512 * bank + n], w, sw, x, sx, True, True)
+
+
+def root_program(g, core, T, topo, calls):
+    v, pe, sc = g.vector, g.tensor, g.scalar
+    cut = 512 * W1CUT
+    K = len(CHUNKS)
+
+    def load_x(q, k):
+        a, b = CHUNKS[k]
+        q.dma_start(T.xt[:, 4 * a:4 * b], T.x[:, 4 * a:4 * b]).then_inc(T.sem["lx%d" % k], 16)
+
+    sc.dma_start(T.w1t[:, :cut], T.w1[:, :cut]).then_inc(T.sem.lw1a, 16)
+    load_x(g.sync, 0)
+    sc.dma_start(T.w1t[:, cut:], T.w1[:, cut:]).then_inc(T.sem.lw1b, 16)
+    for k in range(1, K):
+        load_x(g.sync, k)
+    g.sync.dma_start(T.w2t[:], T.w2[:]).then_inc(T.sem.lw2, 16)
+
+    def quant_w1(i):
+        c = slice(128 * i, 128 * i + 128)
+        v.quantize_mx(T.qw1[:, c], T.sw1[:, c], T.w1t[:, 512 * i:512 * i + 512]).then_inc(
+            T.sem.qw1a if i < W1CUT else T.sem.qw1b, 1)
+
+    def quant_x(k):
+        a, b = CHUNKS[k]
+        v.wait_ge(T.sem["lx%d" % k], 16)
+        v.quantize_mx(T.qx[:, a:b], T.sx[:, a:b], T.xt[:, 4 * a:4 * b]).then_inc(T.sem["qx%d" % k], 1)
+
+    v.wait_ge(T.sem.lw1a, 16)
+    for i in range(W1CUT):
+        quant_w1(i)
+    quant_x(0)
+    v.wait_ge(T.sem.lw1b, 16)
+    for i in range(W1CUT, G):
+        quant_w1(i)
+    wait_pe = waiter(pe, T)
+    for k, (a, b) in enumerate(CHUNKS):
+        n = b - a
+        base = 4 * (k % 2)
+        wait_pe("qw1a", W1CUT)
+        wait_pe("qx%d" % k, 1)
+        if k >= 2:
+            wait_pe("act%d" % (k - 2), G)
+        for i in (0, 2, 1, 3):
+            if i >= W1CUT:
+                wait_pe("qw1b", G - W1CUT)
+            c = slice(128 * i, 128 * i + 128)
+            mm(pe, T, base + i, n, T.qw1[:, c], T.sw1[:, c], T.qx[:, a:b], T.sx[:, a:b]).then_inc(T.sem["z%d_%d" % (k, i)], 1)
+        for i in (0, 1):
+            sc.wait_ge(T.sem["z%d_%d" % (k, i)], 1)
+            sc.activation(T.ht[:, 4 * a + i:4 * b:4], T.ps[:, 512 * (base + i):512 * (base + i) + n],
+                          ActivationFunctionType.Relu, scale=C).then_inc(T.sem["act%d" % k], 1)
+        if k + 1 < K and k not in CFG["xlate"]:
+            quant_x(k + 1)
+        for i in (2, 3):
+            v.wait_ge(T.sem["z%d_%d" % (k, i)], 1)
+            v.tensor_scalar(T.ht[:, 4 * a + i:4 * b:4], T.ps[:, 512 * (base + i):512 * (base + i) + n],
+                            0.0, C, AluOpType.max, AluOpType.mult).then_inc(T.sem["act%d" % k], 1)
+        v.wait_ge(T.sem["act%d" % k], G)
+        v.quantize_mx(T.qh[:, a:b], T.sh[:, a:b], T.ht[:, 4 * a:4 * b]).then_inc(T.sem["qh%d" % k], 1)
+        if k + 1 < K and k in CFG["xlate"]:
+            quant_x(k + 1)
+
+    wait_g = waiter(g, T)
+
+    def made(wait):
+        def ready(item):
+            for k, (a, b) in enumerate(CHUNKS):
+                if a < item[2] and b > item[1]:
+                    wait("qh%d" % k, 1)
+        return ready
+
+    v.wait_ge(T.sem.lw2, 16)
+    v.quantize_mx(T.qw2[:], T.sw2[:], T.w2t[:]).then_inc(T.sem.qw2s, 1)
+    wait_pe("qw2s", 1)
+    for j in range(max(0, K - 2), K):
+        wait_pe("act%d" % j, G)
+    for m, (a, b) in enumerate(TILES):
+        made(wait_pe)(("c", a, b))
+        mm(pe, T, m, NC, T.qw2[:], T.sw2[:], T.qh[:, a:b], T.sh[:, a:b]).then_inc(T.sem["p%d" % m], 1)
+        v.wait_ge(T.sem["p%d" % m], 1)
+        v.tensor_copy(T.yt[:, a:b], T.ps[:, 512 * m:512 * m + NC]).then_inc(T.sem["cp%d" % m], 1)
+        g.sync.wait_ge(T.sem["cp%d" % m], 1)
+        g.sync.dma_start(T.y[:, a:b], T.yt[:, a:b]).then_inc(T.sem.st_sync, 16)
+    g.sync.wait_ge(T.sem.st_sync, 16 * MB)
+    send(g, T, topo, calls[core], made(wait_g))
+
+
+def rank_body(g, core, T, topo, calls):
+    land = landings(calls, core)
+    v, pe, sc = g.vector, g.tensor, g.scalar
+    g.sync.dma_start(T.w2t[:], T.w2[:]).then_inc(T.sem.lw2, 16)
+    v.wait_ge(T.sem.lw2, 16)
+    v.quantize_mx(T.qw2[:], T.sw2[:], T.w2t[:]).then_inc(T.sem.qw2s, 1)
+    wait_pe = waiter(pe, T)
+    wait_pe("qw2s", 1)
+    stores = {"sync": 0, "scal": 0}
+    for y, (ya, yb) in enumerate(cuts(CFG["ygroups"])):
+        mine = [(j, p) for j, p in enumerate(MMS) if ya <= p[0] < yb]
+        on = (g.sync, "sync") if y % 2 == 0 else (sc, "scal")
+        for j, (a, b) in mine:
+            for item, count in land.items():
+                if item[1] < b and item[2] > a:
+                    wait_pe(name(item), count)
+            mm(pe, T, j, b - a, T.qw2[:], T.sw2[:], T.qh[:, a:b], T.sh[:, a:b]).then_inc(T.sem["p%d" % j], 1)
+            src = T.ps[:, 512 * j:512 * j + b - a]
+            if j % 2 == 0:
+                v.wait_ge(T.sem["p%d" % j], 1)
+                v.tensor_copy(T.yt[:, a:b], src).then_inc(T.sem["cp%d" % j], 1)
+            else:
+                sc.wait_ge(T.sem["p%d" % j], 1)
+                sc.activation(T.yt[:, a:b], src, ActivationFunctionType.Copy).then_inc(T.sem["cp%d" % j], 1)
+        for j, _ in mine:
+            on[0].wait_ge(T.sem["cp%d" % j], 1)
+        on[0].dma_start(T.y[:, ya:yb], T.yt[:, ya:yb]).then_inc(T.sem["st_" + on[1]], 16)
+        stores[on[1]] += 16
+    if stores["sync"]:
+        g.sync.wait_ge(T.sem.st_sync, stores["sync"])
+    if stores["scal"]:
+        sc.wait_ge(T.sem.st_scal, stores["scal"])
+
+
+def rank_program(g, core, T, topo):
+    calls = plan(T, topo)
+    root = T.cores[T.root]
+    if core == root:
+        root_program(g, core, T, topo, calls)
+        return
+    land = landings(calls, core)
+    if T.rank_of(core) is not None:
+        rank_body(g, core, T, topo, calls)
+    if core in calls:
+        wait = waiter(g, T)
+        send(g, T, topo, calls[core], lambda item: wait(name(item), land[item]))

@@ -7,15 +7,30 @@ NC, MB, G = 512, 2, 4
 COLS = MB * NC
 C = float(np.float32(0.047))
 
+OFF = ["n0", "f0", "n1", "f1", "n2", "f2", "n3", "f3"]
+
+
+def REST(r):
+    return [x for x in OFF if x != r]
+
+
 CFG = {
     "chunks": [128, 128, 256, 256, 256],
     "pieces": [128] * 8,
-    "relays": [0, 1, 2, 3, 4, 5, 0, 1],
-    "calls": [[0], [1], [2, 3], [4, 5], "s", [6, 7], "c"],
+    "root": [[("c0", "f1")], [("c1", "f2")], [("S0", "a2"), ("S0", "a1"), ("S0", "b0"), ("c3", "f0")], [("c2", "n2")],
+             [("c5", "n0"), ("c4", "n3")], [("c6", "f3")], [("c7", "n1"), ("c7", "b1"), ("S1", "f1"), ("S1", "s")],
+             [("S0", "s")], [("C", "s")]],
+    "relays": [("c0", "f1", REST("f1")), ("c1", "f2", REST("f2")),
+               ("S0", "a2", ["n0", "f1", "n3"]), ("S0", "a1", ["f0", "n2", "f3"]), ("S0", "b0", ["n1", "f2"]),
+               ("c3", "f0", REST("f0")), ("c2", "n2", REST("n2")), ("c5", "n0", REST("n0")), ("c4", "n3", REST("n3")),
+               ("c6", "f3", REST("f3")), ("c7", "n1", ["n0", "f1", "n2", "n3"]), ("c7", "b1", ["f0", "f2", "f3"]),
+               ("S1", "f1", ["n0", "n1", "n2", "n3"]), ("S1", "s", ["f0", "f2", "f3"])],
     "relay_on": 2,
+    "fwd": 4,
     "mms": [256, 256, 128, 128, 128, 128],
-    "ygroups": [512, 256, 256],
-    "xlate": [0],
+    "ygroups": [256, 256, 256, 256],
+    "xlate": [],
+    "scal": [(0, 1, 3)] * 4 + [(0, 1)],
 }
 
 
@@ -38,8 +53,11 @@ def name(item):
     return "%s%d_%d" % item
 
 
-CODES = [("c",) + p for p in PIECES]
-ALL_C, ALL_S = ("c", 0, COLS), ("s", 0, COLS)
+ITEMS = {"C": ("c", 0, COLS), "S": ("s", 0, COLS)}
+for _i, _p in enumerate(PIECES):
+    ITEMS["c%d" % _i] = ("c",) + _p
+for _i, _p in enumerate(TILES):
+    ITEMS["S%d" % _i] = ("s",) + _p
 
 SCRATCH = {
     "xt": ("sbuf", [128, 4 * COLS], "bfloat16"),
@@ -65,7 +83,7 @@ SEMAPHORES = (["lw1a", "lw1b", "lw2", "qw1a", "qw1b", "qw2s", "sent", "st_sync",
               + ["qh%d" % k for k in range(len(CHUNKS))]
               + ["p%d" % k for k in range(8)]
               + ["cp%d" % k for k in range(8)]
-              + [name(i) for i in CODES + [ALL_C, ALL_S]])
+              + [name(i) for i in ITEMS.values()])
 
 
 def bits(mask):
@@ -77,31 +95,38 @@ def plan(T, topo):
     here = topo.chip(root)
     off = [c for c in T.cores if topo.chip(c) != here]
     sib = [c for c in T.cores if topo.chip(c) == here and c != root]
-    near = [c for c in off if topo.die(c) == topo.die(root)]
-    far = [c for c in off if topo.die(c) != topo.die(root)]
     helpers = [c for c in range(SIM_CORES) if topo.chip(c) == here and c not in T.cores
-               and topo.die(c) == topo.die(root) and all(topo.may_write(c, d) for d in off)]
+               and all(topo.may_write(c, d) for d in off)]
     e_off = bits(topo.mask(root, off[0]))
     e_on = [b for b in bits(topo.mask(root, sib[0])) if b not in e_off]
-    order = near + far
-    relay = [order[i] for i in CFG["relays"]]
-    scale_relays = sib + helpers[:1]
+    roles = {"s": sib[0]}
+    for kind, cores, near in (("n", off, True), ("f", off, False), ("a", helpers, True), ("b", helpers, False)):
+        for i, c in enumerate([c for c in cores if (topo.die(c) == topo.die(root)) == near]):
+            roles["%s%d" % (kind, i)] = c
+
+    def share(engines, i, n):
+        k = 1
+        while 2 * k * n <= len(engines):
+            k *= 2
+        return engines[k * i:k * i + k]
+
     calls = {root: []}
-    for call in CFG["calls"]:
-        if call == "s":
-            n = len(e_on) // len(scale_relays)
-            calls[root].append([(ALL_S, [h], e_on[n * i:n * i + n]) for i, h in enumerate(scale_relays)])
-        elif call == "c":
-            calls[root].append([(ALL_C, sib, e_on)])
-        else:
-            n = len(e_off) // len(call)
-            calls[root].append([(CODES[k], [relay[k]], e_off[n * i:n * i + n]) for i, k in enumerate(call)])
-    for k, r in enumerate(relay):
-        on = [c for c in off if c != r and topo.chip(c) == topo.chip(r)]
-        away = [c for c in off if topo.chip(c) != topo.chip(r)]
-        calls.setdefault(r, []).append([(CODES[k], away, e_off), (CODES[k], on, e_on[:CFG["relay_on"]])])
-    for i, h in enumerate(scale_relays):
-        calls.setdefault(h, []).append([(ALL_S, off[i::len(scale_relays)], e_off)])
+    for call in CFG["root"]:
+        away = [x for x in call if roles[x[1]] in off]
+        on = [x for x in call if roles[x[1]] not in off]
+        calls[root].append([(ITEMS[i], [roles[r]], share(e, j, len(part)))
+                            for part, e in ((away, e_off), (on, e_on)) for j, (i, r) in enumerate(part)])
+    for i, r, dests in CFG["relays"]:
+        c = roles[r]
+        d = [roles[x] for x in dests]
+        away = [x for x in d if topo.chip(x) != topo.chip(c)]
+        on = [x for x in d if topo.chip(x) == topo.chip(c)]
+        call = []
+        if away:
+            call.append((ITEMS[i], away, e_off))
+        if on:
+            call.append((ITEMS[i], on, e_on[:CFG["relay_on"] if away else CFG["fwd"]]))
+        calls.setdefault(c, []).append(call)
     return calls
 
 
@@ -200,13 +225,13 @@ def root_program(g, core, T, topo, calls):
                 wait_pe("qw1b", G - W1CUT)
             c = slice(128 * i, 128 * i + 128)
             mm(pe, T, base + i, n, T.qw1[:, c], T.sw1[:, c], T.qx[:, a:b], T.sx[:, a:b]).then_inc(T.sem["z%d_%d" % (k, i)], 1)
-        for i in (0, 1):
+        for i in CFG["scal"][k]:
             sc.wait_ge(T.sem["z%d_%d" % (k, i)], 1)
             sc.activation(T.ht[:, 4 * a + i:4 * b:4], T.ps[:, 512 * (base + i):512 * (base + i) + n],
                           ActivationFunctionType.Relu, scale=C).then_inc(T.sem["act%d" % k], 1)
         if k + 1 < K and k not in CFG["xlate"]:
             quant_x(k + 1)
-        for i in (2, 3):
+        for i in [i for i in range(G) if i not in CFG["scal"][k]]:
             v.wait_ge(T.sem["z%d_%d" % (k, i)], 1)
             v.tensor_scalar(T.ht[:, 4 * a + i:4 * b:4], T.ps[:, 512 * (base + i):512 * (base + i) + n],
                             0.0, C, AluOpType.max, AluOpType.mult).then_inc(T.sem["act%d" % k], 1)

@@ -7,29 +7,25 @@ NC, MB, G = 512, 2, 4
 COLS = MB * NC
 C = float(np.float32(0.047))
 
-OFF = ["n0", "f0", "n1", "f1", "n2", "f2", "n3", "f3"]
-
-
-def REST(r):
-    return [x for x in OFF if x != r]
-
-
 CFG = {
     "chunks": [128, 128, 256, 256, 256],
     "pieces": [128] * 8,
-    "root": [[("c0", "f1")], [("c1", "f2")], [("S0", "a2"), ("S0", "a1"), ("S0", "b0"), ("c3", "f0")], [("c2", "n2")],
-             [("c5", "n0"), ("c4", "n3")], [("c6", "f3")], [("c7", "n1"), ("c7", "b1"), ("S1", "f1"), ("S1", "s")],
-             [("S0", "s")], [("C", "s")]],
-    "relays": [("c0", "f1", REST("f1")), ("c1", "f2", REST("f2")),
-               ("S0", "a2", ["n0", "f1", "n3"]), ("S0", "a1", ["f0", "n2", "f3"]), ("S0", "b0", ["n1", "f2"]),
-               ("c3", "f0", REST("f0")), ("c2", "n2", REST("n2")), ("c5", "n0", REST("n0")), ("c4", "n3", REST("n3")),
-               ("c6", "f3", REST("f3")), ("c7", "n1", ["n0", "f1", "n2", "n3"]), ("c7", "b1", ["f0", "f2", "f3"]),
-               ("S1", "f1", ["n0", "n1", "n2", "n3"]), ("S1", "s", ["f0", "f2", "f3"])],
-    "relay_on": 2,
-    "fwd": 4,
+    "planes": [512, 512],
+    "root": [[("c0", "F1")], [("c1", "N2")], [("S0", "a2 b0 s"), ("c3", "F0")], [("c2", "N3")],
+             [("c4", "N1"), ("c5", "F2")], [("c6", "F3 a1")], [("c7", "N0 b1"), ("S1", "s F1")], [("C", "s")]],
+    "held": ["C"],
+    "relays": [("c1", "N2", "n0 n1 n2 f2 n3"), ("c0", "F1", "f0 f1 n1 f2 f3"), ("S0", "a2", "n0 n3"),
+               ("c2", "N3", "n0 n1 n2 n3 f3"), ("S0", "b0", "f1 f2"), ("c3", "F0", "f0 n0 f1 f2 f3"),
+               ("c1", "n0", "f0"), ("c4", "N1", "n0 n1 f1 n2 n3"), ("c5", "F2", "f0 f1 f2 n2 f3"), ("c0", "f0", "n0"),
+               ("c1", "n1", "f1"), ("c6", "a1", "n0 n1 n2"), ("c0", "f2", "n2"), ("S0", "n0", "f0"),
+               ("c6", "F3", "f0 f1 f2 f3 n3"), ("c0", "f3", "n3"), ("c7", "b1", "f1 f2 f3"), ("S1", "s", "f0 f2 f3"),
+               ("c1", "n3", "f3"), ("S0", "f1", "n1"), ("S1", "F1", "n0 n2 n3 n1 f1"), ("c7", "N0", "n1 n2 n3 n0 f0"),
+               ("S0", "f2", "n2"), ("S0", "n3", "f3"), ("c3", "f1", "n1"), ("c2", "n0", "f0"), ("c3", "f2", "n2"),
+               ("c2", "n1", "f1"), ("c5", "f0", "n0"), ("c4", "n0", "f0"), ("c3", "f3", "n3"), ("c5", "f1", "n1"),
+               ("c2", "n2", "f2"), ("c4", "n2", "f2"), ("c5", "f3", "n3"), ("c4", "n3", "f3")],
+    "both": 4,
     "mms": [256, 256, 128, 128, 128, 128],
     "ygroups": [256, 256, 256, 256],
-    "xlate": [],
     "scal": [(0, 1, 3)] * 4 + [(0, 1)],
 }
 
@@ -43,7 +39,6 @@ def cuts(widths):
 
 
 CHUNKS = cuts(CFG["chunks"])
-PIECES = cuts(CFG["pieces"])
 MMS = cuts(CFG["mms"])
 TILES = cuts([NC] * MB)
 W1CUT = 3
@@ -53,10 +48,10 @@ def name(item):
     return "%s%d_%d" % item
 
 
-ITEMS = {"C": ("c", 0, COLS), "S": ("s", 0, COLS)}
-for _i, _p in enumerate(PIECES):
+ITEMS = {"C": ("c", 0, COLS)}
+for _i, _p in enumerate(cuts(CFG["pieces"])):
     ITEMS["c%d" % _i] = ("c",) + _p
-for _i, _p in enumerate(TILES):
+for _i, _p in enumerate(cuts(CFG["planes"])):
     ITEMS["S%d" % _i] = ("s",) + _p
 
 SCRATCH = {
@@ -95,14 +90,17 @@ def plan(T, topo):
     here = topo.chip(root)
     off = [c for c in T.cores if topo.chip(c) != here]
     sib = [c for c in T.cores if topo.chip(c) == here and c != root]
-    helpers = [c for c in range(SIM_CORES) if topo.chip(c) == here and c not in T.cores
-               and all(topo.may_write(c, d) for d in off)]
+    idle = [c for c in range(SIM_CORES) if c not in T.cores and all(topo.may_write(c, d) for d in off)]
     e_off = bits(topo.mask(root, off[0]))
     e_on = [b for b in bits(topo.mask(root, sib[0])) if b not in e_off]
-    roles = {"s": sib[0]}
-    for kind, cores, near in (("n", off, True), ("f", off, False), ("a", helpers, True), ("b", helpers, False)):
-        for i, c in enumerate([c for c in cores if (topo.die(c) == topo.die(root)) == near]):
-            roles["%s%d" % (kind, i)] = c
+    roles = {"root": root, "s": sib[0]}
+    for near, rank, helper in ((True, "n", "a"), (False, "f", "b")):
+        mine = [c for c in idle if (topo.die(c) == topo.die(root)) == near]
+        for i, c in enumerate([c for c in mine if topo.chip(c) == here]):
+            roles["%s%d" % (helper, i)] = c
+        for i, c in enumerate([c for c in off if (topo.die(c) == topo.die(root)) == near]):
+            roles["%s%d" % (rank, i)] = c
+            roles["%s%d" % (rank.upper(), i)] = [h for h in mine if topo.chip(h) == topo.chip(c)][0]
 
     def share(engines, i, n):
         k = 1
@@ -110,23 +108,20 @@ def plan(T, topo):
             k *= 2
         return engines[k * i:k * i + k]
 
-    calls = {root: []}
-    for call in CFG["root"]:
-        away = [x for x in call if roles[x[1]] in off]
-        on = [x for x in call if roles[x[1]] not in off]
-        calls[root].append([(ITEMS[i], [roles[r]], share(e, j, len(part)))
-                            for part, e in ((away, e_off), (on, e_on)) for j, (i, r) in enumerate(part)])
+    def call(c, sends):
+        parts = [(i, [roles[r] for r in rs.split()]) for i, rs in sends]
+        away = [(i, [d for d in ds if topo.chip(d) != topo.chip(c)]) for i, ds in parts]
+        on = [(i, [d for d in ds if topo.chip(d) == topo.chip(c)]) for i, ds in parts]
+        away, on = [p for p in away if p[1]], [p for p in on if p[1]]
+        e = e_on[:CFG["both"]] if away and c != root else e_on
+        if sends[0][0] in CFG["held"]:
+            e = e_on + e_off
+        return [(ITEMS[i], ds, share(engines, j, len(part)))
+                for part, engines in ((away, e_off), (on, e)) for j, (i, ds) in enumerate(part)]
+
+    calls = {root: [call(root, sends) for sends in CFG["root"]]}
     for i, r, dests in CFG["relays"]:
-        c = roles[r]
-        d = [roles[x] for x in dests]
-        away = [x for x in d if topo.chip(x) != topo.chip(c)]
-        on = [x for x in d if topo.chip(x) == topo.chip(c)]
-        call = []
-        if away:
-            call.append((ITEMS[i], away, e_off))
-        if on:
-            call.append((ITEMS[i], on, e_on[:CFG["relay_on"] if away else CFG["fwd"]]))
-        calls.setdefault(c, []).append(call)
+        calls.setdefault(roles[r], []).append(call(roles[r], [(i, dests)]))
     return calls
 
 
@@ -148,8 +143,11 @@ def view(T, item):
 
 def send(g, T, topo, calls, ready):
     total = 0
+    held = [ITEMS[i] for i in CFG["held"]]
     for call in calls:
         transfers = []
+        if call[0][0] in held:
+            g.wait_ge(T.sem.sent, total)
         for item, dsts, engines in call:
             ready(item)
             ids = []
@@ -229,7 +227,7 @@ def root_program(g, core, T, topo, calls):
             sc.wait_ge(T.sem["z%d_%d" % (k, i)], 1)
             sc.activation(T.ht[:, 4 * a + i:4 * b:4], T.ps[:, 512 * (base + i):512 * (base + i) + n],
                           ActivationFunctionType.Relu, scale=C).then_inc(T.sem["act%d" % k], 1)
-        if k + 1 < K and k not in CFG["xlate"]:
+        if k + 1 < K:
             quant_x(k + 1)
         for i in [i for i in range(G) if i not in CFG["scal"][k]]:
             v.wait_ge(T.sem["z%d_%d" % (k, i)], 1)
@@ -237,8 +235,6 @@ def root_program(g, core, T, topo, calls):
                             0.0, C, AluOpType.max, AluOpType.mult).then_inc(T.sem["act%d" % k], 1)
         v.wait_ge(T.sem["act%d" % k], G)
         v.quantize_mx(T.qh[:, a:b], T.sh[:, a:b], T.ht[:, 4 * a:4 * b]).then_inc(T.sem["qh%d" % k], 1)
-        if k + 1 < K and k in CFG["xlate"]:
-            quant_x(k + 1)
 
     wait_g = waiter(g, T)
 
@@ -260,9 +256,11 @@ def root_program(g, core, T, topo, calls):
         v.wait_ge(T.sem["p%d" % m], 1)
         v.tensor_copy(T.yt[:, a:b], T.ps[:, 512 * m:512 * m + NC]).then_inc(T.sem["cp%d" % m], 1)
         g.sync.wait_ge(T.sem["cp%d" % m], 1)
+    send(g, T, topo, calls[core], made(wait_g))
+    g.sync.wait_ge(T.sem.sent, sum(len(e) for call in calls[core] for _, _, e in call))
+    for a, b in TILES:
         g.sync.dma_start(T.y[:, a:b], T.yt[:, a:b]).then_inc(T.sem.st_sync, 16)
     g.sync.wait_ge(T.sem.st_sync, 16 * MB)
-    send(g, T, topo, calls[core], made(wait_g))
 
 
 def rank_body(g, core, T, topo, calls):

@@ -10,23 +10,25 @@ C = float(np.float32(0.047))
 CFG = {
     "chunks": [128, 128, 256, 256, 256],
     "pieces": [128] * 8,
-    "planes": [512, 512],
-    "root": [[("c0", "F1")], [("c1", "N2")], [("S0", "a2 b0 s"), ("c3", "F0")], [("c2", "N3")],
-             [("c4", "N1"), ("c5", "F2")], [("c6", "F3 a1")], [("c7", "N0 b1"), ("S1", "s F1")], [("C", "s")]],
+    "planes": [512, 256, 256],
+    "root": [[("c0", "b2")], [("c1", "N0")], [("S0", "N3 s"), ("c3", "F0")], [("c2", "a2 b0")], [("S1", "s")],
+             [("c5", "F3")], [("c4", "N0")], [("S2", "a0 s")], [("c6", "N3 b2"), ("c7", "a1 F0")], [("C", "s")]],
     "held": ["C"],
-    "relays": [("c1", "N2", "n0 n1 n2 f2 n3"), ("c0", "F1", "f0 f1 n1 f2 f3"), ("S0", "a2", "n0 n3"),
-               ("c2", "N3", "n0 n1 n2 n3 f3"), ("S0", "b0", "f1 f2"), ("c3", "F0", "f0 n0 f1 f2 f3"),
-               ("c1", "n0", "f0"), ("c4", "N1", "n0 n1 f1 n2 n3"), ("c5", "F2", "f0 f1 f2 n2 f3"), ("c0", "f0", "n0"),
-               ("c1", "n1", "f1"), ("c6", "a1", "n0 n1 n2"), ("c0", "f2", "n2"), ("S0", "n0", "f0"),
-               ("c6", "F3", "f0 f1 f2 f3 n3"), ("c0", "f3", "n3"), ("c7", "b1", "f1 f2 f3"), ("S1", "s", "f0 f2 f3"),
-               ("c1", "n3", "f3"), ("S0", "f1", "n1"), ("S1", "F1", "n0 n2 n3 n1 f1"), ("c7", "N0", "n1 n2 n3 n0 f0"),
-               ("S0", "f2", "n2"), ("S0", "n3", "f3"), ("c3", "f1", "n1"), ("c2", "n0", "f0"), ("c3", "f2", "n2"),
-               ("c2", "n1", "f1"), ("c5", "f0", "n0"), ("c4", "n0", "f0"), ("c3", "f3", "n3"), ("c5", "f1", "n1"),
-               ("c2", "n2", "f2"), ("c4", "n2", "f2"), ("c5", "f3", "n3"), ("c4", "n3", "f3")],
-    "both": 4,
+    "relays": [("c0", "b2", "f0 f1 f2 f3"), ("c1", "N0", "n0 f0 n1 n2 n3"), ("c2", "a2", "n0 n3"),
+               ("S0", "N3", "n0 n1 n2 n3 f3"), ("c3", "F0", "f0 n0 f1 f2 f3"), ("c2", "b0", "f1 f2"),
+               ("c0", "f0", "n0"), ("S1", "s", "f0 f1 f2 f3"), ("c5", "F3", "f0 f1 f2 f3 n3"),
+               ("S2", "a0", "n0 n1 n2 n3"), ("c0", "f1", "n1"), ("c4", "N0", "n0 f0 n1 n2 n3"), ("c1", "n1", "f1"),
+               ("c0", "f2", "n2"), ("c1", "n2", "f2"), ("c6", "N3", "n0 n1 n2 n3"), ("c0", "f3", "n3"),
+               ("c7", "F0", "f1 f2 f3 f0 n0"), ("c6", "b2", "f0 f1 f2 f3"), ("c7", "a1", "n3 n1 n2"),
+               ("c1", "n3", "f3"), ("c2", "n0", "f0"), ("c3", "f1", "n1"), ("S1", "f0", "n0"), ("c4", "n1", "f1"),
+               ("c2", "n3", "f3"), ("S0", "n0", "f0"), ("c3", "f2", "n2"), ("c2", "f1", "n1"), ("c4", "n2", "f2"),
+               ("c5", "f0", "n0"), ("S2", "n0", "f0"), ("S0", "n1", "f1"), ("S1", "f1", "n1"), ("c3", "f3", "n3"),
+               ("S2", "n1", "f1"), ("c4", "n3", "f3"), ("c2", "f2", "n2"), ("S0", "n2", "f2"), ("S1", "f2", "n2"),
+               ("c5", "f1", "n1"), ("S2", "n2", "f2"), ("c5", "f2", "n2"), ("S1", "f3", "n3"), ("S2", "n3", "f3")],
+    "both": 8,
     "mms": [256, 256, 128, 128, 128, 128],
     "ygroups": [256, 256, 256, 256],
-    "scal": [(0, 1, 3)] * 4 + [(0, 1)],
+    "scal": [(0, 1, 3), (0, 1, 3), (0, 1), (0, 1, 3), (0, 1)],
 }
 
 
@@ -113,9 +115,10 @@ def plan(T, topo):
         away = [(i, [d for d in ds if topo.chip(d) != topo.chip(c)]) for i, ds in parts]
         on = [(i, [d for d in ds if topo.chip(d) == topo.chip(c)]) for i, ds in parts]
         away, on = [p for p in away if p[1]], [p for p in on if p[1]]
-        e = e_on[:CFG["both"]] if away and c != root else e_on
-        if sends[0][0] in CFG["held"]:
+        if sends[0][0] in CFG["held"] or (c != root and not away):
             e = e_on + e_off
+        else:
+            e = e_on if c == root else e_on[:CFG["both"]]
         return [(ITEMS[i], ds, share(engines, j, len(part)))
                 for part, engines in ((away, e_off), (on, e)) for j, (i, ds) in enumerate(part)]
 

import numpy as np
from concourse.bass import DstId, RemoteDMATransfer
from concourse.mybir import dt, AluOpType, ActivationFunctionType

SIM_CORES = 80
NC, MB, G = 512, 2, 4
COLS = MB * NC
C = float(np.float32(0.047))

CFG = {
    "chunks": [128, 128, 256, 256, 256],
    "pieces": [128] * 8,
    "planes": [512, 256, 256],
    "root": [[("c0", "b2")], [("c1", "N0")], [("S0", "N3 s"), ("c3", "F0")], [("c2", "a2 b0")], [("S1", "s")],
             [("c5", "F3")], [("c4", "N0")], [("S2", "a0 s")], [("c6", "N3 b2"), ("c7", "a1 F0")], [("C", "s")]],
    "held": ["C"],
    "relays": [("c0", "b2", "f0 f1 f2 f3"), ("c1", "N0", "n0 f0 n1 n2 n3"), ("c2", "a2", "n0 n3"),
               ("S0", "N3", "n0 n1 n2 n3 f3"), ("c3", "F0", "f0 n0 f1 f2 f3"), ("c2", "b0", "f1 f2"),
               ("c0", "f0", "n0"), ("S1", "s", "f0 f1 f2 f3"), ("c5", "F3", "f0 f1 f2 f3 n3"),
               ("S2", "a0", "n0 n1 n2 n3"), ("c0", "f1", "n1"), ("c4", "N0", "n0 f0 n1 n2 n3"), ("c1", "n1", "f1"),
               ("c0", "f2", "n2"), ("c1", "n2", "f2"), ("c6", "N3", "n0 n1 n2 n3"), ("c0", "f3", "n3"),
               ("c7", "F0", "f1 f2 f3 f0 n0"), ("c6", "b2", "f0 f1 f2 f3"), ("c7", "a1", "n3 n1 n2"),
               ("c1", "n3", "f3"), ("c2", "n0", "f0"), ("c3", "f1", "n1"), ("S1", "f0", "n0"), ("c4", "n1", "f1"),
               ("c2", "n3", "f3"), ("S0", "n0", "f0"), ("c3", "f2", "n2"), ("c2", "f1", "n1"), ("c4", "n2", "f2"),
               ("c5", "f0", "n0"), ("S2", "n0", "f0"), ("S0", "n1", "f1"), ("S1", "f1", "n1"), ("c3", "f3", "n3"),
               ("S2", "n1", "f1"), ("c4", "n3", "f3"), ("c2", "f2", "n2"), ("S0", "n2", "f2"), ("S1", "f2", "n2"),
               ("c5", "f1", "n1"), ("S2", "n2", "f2"), ("c5", "f2", "n2"), ("S1", "f3", "n3"), ("S2", "n3", "f3")],
    "both": 8,
    "mms": [256, 256, 128, 128, 128, 128],
    "ygroups": [256, 256, 256, 256],
    "scal": [(0, 1, 3), (0, 1, 3), (0, 1), (0, 1, 3), (0, 1)],
}


def cuts(widths):
    out, a = [], 0
    for w in widths:
        out.append((a, a + w))
        a += w
    return out


CHUNKS = cuts(CFG["chunks"])
MMS = cuts(CFG["mms"])
TILES = cuts([NC] * MB)
W1CUT = 3


def name(item):
    return "%s%d_%d" % item


ITEMS = {"C": ("c", 0, COLS)}
for _i, _p in enumerate(cuts(CFG["pieces"])):
    ITEMS["c%d" % _i] = ("c",) + _p
for _i, _p in enumerate(cuts(CFG["planes"])):
    ITEMS["S%d" % _i] = ("s",) + _p

SCRATCH = {
    "xt": ("sbuf", [128, 4 * COLS], "bfloat16"),
    "w1t": ("sbuf", [128, 4 * 128 * G], "bfloat16"),
    "w2t": ("sbuf", [128, 4 * 128], "bfloat16"),
    "ht": ("sbuf", [128, 4 * COLS], "bfloat16"),
    "qx": ("sbuf", [128, COLS], "float8_e4m3fn_x4"),
    "sx": ("sbuf", [128, COLS], "uint8"),
    "qw1": ("sbuf", [128, 128 * G], "float8_e4m3fn_x4"),
    "sw1": ("sbuf", [128, 128 * G], "uint8"),
    "qw2": ("sbuf", [128, 128], "float8_e4m3fn_x4"),
    "sw2": ("sbuf", [128, 128], "uint8"),
    "qh": ("sbuf", [128, COLS], "float8_e4m3fn_x4"),
    "sh": ("sbuf", [128, COLS], "uint8"),
    "yt": ("sbuf", [128, COLS], "float32"),
    "ps": ("psum", [128, 512 * 8], "float32"),
}
SEMAPHORES = (["lw1a", "lw1b", "lw2", "qw1a", "qw1b", "qw2s", "sent", "st_sync", "st_scal"]
              + ["lx%d" % k for k in range(len(CHUNKS))]
              + ["qx%d" % k for k in range(len(CHUNKS))]
              + ["z%d_%d" % (k, b) for k in range(len(CHUNKS)) for b in range(G)]
              + ["act%d" % k for k in range(len(CHUNKS))]
              + ["qh%d" % k for k in range(len(CHUNKS))]
              + ["p%d" % k for k in range(8)]
              + ["cp%d" % k for k in range(8)]
              + [name(i) for i in ITEMS.values()])


def bits(mask):
    return [1 << i for i in range(16) if mask >> i & 1]


def plan(T, topo):
    root = T.cores[T.root]
    here = topo.chip(root)
    off = [c for c in T.cores if topo.chip(c) != here]
    sib = [c for c in T.cores if topo.chip(c) == here and c != root]
    idle = [c for c in range(SIM_CORES) if c not in T.cores and all(topo.may_write(c, d) for d in off)]
    e_off = bits(topo.mask(root, off[0]))
    e_on = [b for b in bits(topo.mask(root, sib[0])) if b not in e_off]
    roles = {"root": root, "s": sib[0]}
    for near, rank, helper in ((True, "n", "a"), (False, "f", "b")):
        mine = [c for c in idle if (topo.die(c) == topo.die(root)) == near]
        for i, c in enumerate([c for c in mine if topo.chip(c) == here]):
            roles["%s%d" % (helper, i)] = c
        for i, c in enumerate([c for c in off if (topo.die(c) == topo.die(root)) == near]):
            roles["%s%d" % (rank, i)] = c
            roles["%s%d" % (rank.upper(), i)] = [h for h in mine if topo.chip(h) == topo.chip(c)][0]

    def share(engines, i, n):
        k = 1
        while 2 * k * n <= len(engines):
            k *= 2
        return engines[k * i:k * i + k]

    def call(c, sends):
        parts = [(i, [roles[r] for r in rs.split()]) for i, rs in sends]
        away = [(i, [d for d in ds if topo.chip(d) != topo.chip(c)]) for i, ds in parts]
        on = [(i, [d for d in ds if topo.chip(d) == topo.chip(c)]) for i, ds in parts]
        away, on = [p for p in away if p[1]], [p for p in on if p[1]]
        if sends[0][0] in CFG["held"] or (c != root and not away):
            e = e_on + e_off
        else:
            e = e_on if c == root else e_on[:CFG["both"]]
        return [(ITEMS[i], ds, share(engines, j, len(part)))
                for part, engines in ((away, e_off), (on, e)) for j, (i, ds) in enumerate(part)]

    calls = {root: [call(root, sends) for sends in CFG["root"]]}
    for i, r, dests in CFG["relays"]:
        calls.setdefault(roles[r], []).append(call(roles[r], [(i, dests)]))
    return calls


def landings(calls, core):
    out = {}
    for L in calls.values():
        for call in L:
            for item, dsts, engines in call:
                for d in dsts:
                    if d == core:
                        out[item] = out.get(item, 0) + len(engines)
    return out


def view(T, item):
    kind, a, b = item
    return T.qh[:, a:b].bitcast(dt.uint8) if kind == "c" else T.sh[:, a:b]


def send(g, T, topo, calls, ready):
    total = 0
    held = [ITEMS[i] for i in CFG["held"]]
    for call in calls:
        transfers = []
        if call[0][0] in held:
            g.wait_ge(T.sem.sent, total)
        for item, dsts, engines in call:
            ready(item)
            ids = []
            for d in dsts:
                rid, pid, _ = topo.addr(d)
                ids.append(DstId(rid=rid, pnc=pid))
            transfers.append(RemoteDMATransfer(
                dst_ids=ids, dma_engine_mask=sum(engines), remote_sem=T.sem[name(item)],
                srcs=[view(T, item)], dsts=[view(T, item) for _ in dsts]))
            total += len(engines)
        g.remote_dma_fused(transfers, local_sem=T.sem.sent)
    if total:
        g.wait_ge(T.sem.sent, total)


def waiter(queue, T):
    seen = {}

    def wait(sem, val):
        if seen.get(sem, 0) < val:
            seen[sem] = val
            queue.wait_ge(T.sem[sem], val)
    return wait


def mm(q, T, bank, n, w, sw, x, sx):
    return q.matmul_mx(T.ps[:, 512 * bank:512 * bank + n], w, sw, x, sx, True, True)


def root_program(g, core, T, topo, calls):
    v, pe, sc = g.vector, g.tensor, g.scalar
    cut = 512 * W1CUT
    K = len(CHUNKS)

    def load_x(q, k):
        a, b = CHUNKS[k]
        q.dma_start(T.xt[:, 4 * a:4 * b], T.x[:, 4 * a:4 * b]).then_inc(T.sem["lx%d" % k], 16)

    sc.dma_start(T.w1t[:, :cut], T.w1[:, :cut]).then_inc(T.sem.lw1a, 16)
    load_x(g.sync, 0)
    sc.dma_start(T.w1t[:, cut:], T.w1[:, cut:]).then_inc(T.sem.lw1b, 16)
    for k in range(1, K):
        load_x(g.sync, k)
    g.sync.dma_start(T.w2t[:], T.w2[:]).then_inc(T.sem.lw2, 16)

    def quant_w1(i):
        c = slice(128 * i, 128 * i + 128)
        v.quantize_mx(T.qw1[:, c], T.sw1[:, c], T.w1t[:, 512 * i:512 * i + 512]).then_inc(
            T.sem.qw1a if i < W1CUT else T.sem.qw1b, 1)

    def quant_x(k):
        a, b = CHUNKS[k]
        v.wait_ge(T.sem["lx%d" % k], 16)
        v.quantize_mx(T.qx[:, a:b], T.sx[:, a:b], T.xt[:, 4 * a:4 * b]).then_inc(T.sem["qx%d" % k], 1)

    v.wait_ge(T.sem.lw1a, 16)
    for i in range(W1CUT):
        quant_w1(i)
    quant_x(0)
    v.wait_ge(T.sem.lw1b, 16)
    for i in range(W1CUT, G):
        quant_w1(i)
    wait_pe = waiter(pe, T)
    for k, (a, b) in enumerate(CHUNKS):
        n = b - a
        base = 4 * (k % 2)
        wait_pe("qw1a", W1CUT)
        wait_pe("qx%d" % k, 1)
        if k >= 2:
            wait_pe("act%d" % (k - 2), G)
        for i in (0, 2, 1, 3):
            if i >= W1CUT:
                wait_pe("qw1b", G - W1CUT)
            c = slice(128 * i, 128 * i + 128)
            mm(pe, T, base + i, n, T.qw1[:, c], T.sw1[:, c], T.qx[:, a:b], T.sx[:, a:b]).then_inc(T.sem["z%d_%d" % (k, i)], 1)
        for i in CFG["scal"][k]:
            sc.wait_ge(T.sem["z%d_%d" % (k, i)], 1)
            sc.activation(T.ht[:, 4 * a + i:4 * b:4], T.ps[:, 512 * (base + i):512 * (base + i) + n],
                          ActivationFunctionType.Relu, scale=C).then_inc(T.sem["act%d" % k], 1)
        if k + 1 < K:
            quant_x(k + 1)
        for i in [i for i in range(G) if i not in CFG["scal"][k]]:
            v.wait_ge(T.sem["z%d_%d" % (k, i)], 1)
            v.tensor_scalar(T.ht[:, 4 * a + i:4 * b:4], T.ps[:, 512 * (base + i):512 * (base + i) + n],
                            0.0, C, AluOpType.max, AluOpType.mult).then_inc(T.sem["act%d" % k], 1)
        v.wait_ge(T.sem["act%d" % k], G)
        v.quantize_mx(T.qh[:, a:b], T.sh[:, a:b], T.ht[:, 4 * a:4 * b]).then_inc(T.sem["qh%d" % k], 1)

    wait_g = waiter(g, T)

    def made(wait):
        def ready(item):
            for k, (a, b) in enumerate(CHUNKS):
                if a < item[2] and b > item[1]:
                    wait("qh%d" % k, 1)
        return ready

    v.wait_ge(T.sem.lw2, 16)
    v.quantize_mx(T.qw2[:], T.sw2[:], T.w2t[:]).then_inc(T.sem.qw2s, 1)
    wait_pe("qw2s", 1)
    for j in range(max(0, K - 2), K):
        wait_pe("act%d" % j, G)
    for m, (a, b) in enumerate(TILES):
        made(wait_pe)(("c", a, b))
        mm(pe, T, m, NC, T.qw2[:], T.sw2[:], T.qh[:, a:b], T.sh[:, a:b]).then_inc(T.sem["p%d" % m], 1)
        v.wait_ge(T.sem["p%d" % m], 1)
        v.tensor_copy(T.yt[:, a:b], T.ps[:, 512 * m:512 * m + NC]).then_inc(T.sem["cp%d" % m], 1)
        g.sync.wait_ge(T.sem["cp%d" % m], 1)
    send(g, T, topo, calls[core], made(wait_g))
    g.sync.wait_ge(T.sem.sent, sum(len(e) for call in calls[core] for _, _, e in call))
    for a, b in TILES:
        g.sync.dma_start(T.y[:, a:b], T.yt[:, a:b]).then_inc(T.sem.st_sync, 16)
    g.sync.wait_ge(T.sem.st_sync, 16 * MB)


def rank_body(g, core, T, topo, calls):
    land = landings(calls, core)
    v, pe, sc = g.vector, g.tensor, g.scalar
    g.sync.dma_start(T.w2t[:], T.w2[:]).then_inc(T.sem.lw2, 16)
    v.wait_ge(T.sem.lw2, 16)
    v.quantize_mx(T.qw2[:], T.sw2[:], T.w2t[:]).then_inc(T.sem.qw2s, 1)
    wait_pe = waiter(pe, T)
    wait_pe("qw2s", 1)
    stores = {"sync": 0, "scal": 0}
    for y, (ya, yb) in enumerate(cuts(CFG["ygroups"])):
        mine = [(j, p) for j, p in enumerate(MMS) if ya <= p[0] < yb]
        on = (g.sync, "sync") if y % 2 == 0 else (sc, "scal")
        for j, (a, b) in mine:
            for item, count in land.items():
                if item[1] < b and item[2] > a:
                    wait_pe(name(item), count)
            mm(pe, T, j, b - a, T.qw2[:], T.sw2[:], T.qh[:, a:b], T.sh[:, a:b]).then_inc(T.sem["p%d" % j], 1)
            src = T.ps[:, 512 * j:512 * j + b - a]
            if j % 2 == 0:
                v.wait_ge(T.sem["p%d" % j], 1)
                v.tensor_copy(T.yt[:, a:b], src).then_inc(T.sem["cp%d" % j], 1)
            else:
                sc.wait_ge(T.sem["p%d" % j], 1)
                sc.activation(T.yt[:, a:b], src, ActivationFunctionType.Copy).then_inc(T.sem["cp%d" % j], 1)
        for j, _ in mine:
            on[0].wait_ge(T.sem["cp%d" % j], 1)
        on[0].dma_start(T.y[:, ya:yb], T.yt[:, ya:yb]).then_inc(T.sem["st_" + on[1]], 16)
        stores[on[1]] += 16
    if stores["sync"]:
        g.sync.wait_ge(T.sem.st_sync, stores["sync"])
    if stores["scal"]:
        sc.wait_ge(T.sem.st_scal, stores["scal"])


def rank_program(g, core, T, topo):
    calls = plan(T, topo)
    root = T.cores[T.root]
    if core == root:
        root_program(g, core, T, topo, calls)
        return
    land = landings(calls, core)
    if T.rank_of(core) is not None:
        rank_body(g, core, T, topo, calls)
    if core in calls:
        wait = waiter(g, T)
        send(g, T, topo, calls[core], lambda item: wait(name(item), land[item]))
